import numpy as np
import ml_dtypes


def mxq(x, axis, fmt="e4m3"):
    dtype, down = {"e4m3": (ml_dtypes.float8_e4m3fn, 7), "e5m2": (ml_dtypes.float8_e5m2, 14)}[fmt]
    v = np.moveaxis(np.asarray(x, np.float32).astype(ml_dtypes.bfloat16).astype(np.float64), axis, -1)
    blocks = v.reshape(v.shape[:-1] + (-1, 32))
    amax = np.abs(blocks).max(-1, keepdims=True)
    byte = np.maximum(np.where(amax > 0, np.frexp(amax)[1] - 1 + 127, 0) - down, 1)
    scale = np.exp2(byte - 127.0)
    codes = (blocks / scale).astype(np.float32).astype(dtype).astype(np.float64)
    return np.moveaxis((codes * scale).reshape(v.shape), -1, axis)


WIDE = False


def mx_kscale(k):
    if not WIDE:
        return np.ones(k)
    levels = np.array([10, -10, 5, -5, 0])
    if k % 512:
        return np.exp2(np.random.permutation(np.resize(levels, k // 32))).repeat(32)
    a = np.empty((k // 512, 16))
    for p in range(k // 512):
        a[p, :8] = np.random.permutation(np.resize(levels, 8))
        for g in range(8):
            far = levels[np.abs(levels - a[p, g]) >= 10]
            a[p, g + 8] = far[np.random.randint(len(far))]
    return np.exp2(a.ravel()).repeat(32)


def f64(x):
    return np.asarray(x).astype(np.float64)


def striped(idx):
    return np.tile(idx.reshape(-1, 16).T, (8, 1)).astype(np.uint16)


def unstriped(offs):
    return offs[:16].T.reshape(-1).astype(np.int64)


def striped8(idx):
    return np.concatenate([x.reshape(-1, 16).T for x in idx]).astype(np.uint16)


def runs(offs, k):
    lists = np.stack([offs[16 * r : 16 * r + 16].T.reshape(-1) for r in range(8)]).astype(np.int64)
    return lists[np.arange(k) % 512 // 64]


def pack_weight(w):
    k, n = w.shape
    w = f64(np.asarray(w, np.float32).astype(ml_dtypes.bfloat16)).reshape(k // 32, 32, n)
    amax = np.abs(w).max(1)
    byte = np.clip(np.where(amax > 0, np.frexp(amax)[1] - 1 + 127 - 7, 1), 1, 254)
    scaled = (w * np.exp2(127.0 - byte)[:, None, :]).reshape(k, n).astype(np.float32)
    words = np.ascontiguousarray(scaled.reshape(k // 512, 128, 4, n).transpose(0, 1, 3, 2)).astype(ml_dtypes.float8_e4m3fn).view(np.uint8)
    return words, np.ascontiguousarray(byte.astype(np.uint8).reshape(k // 512, 16, n))


def unpack_weight(words, scales):
    g, p, n, _ = words.shape
    vals = np.ascontiguousarray(words).view(ml_dtypes.float8_e4m3fn).astype(np.float64) * np.repeat(np.exp2(scales.astype(np.float64) - 127.0), 8, axis=1)[..., None]
    return vals.transpose(0, 1, 3, 2).reshape(g * 512, n)


def sigmoid(v):
    return 1.0 / (1.0 + np.exp(-np.maximum(v, -700.0)))


K, T, S, V, N, H, U = 512, 2048, 512, 512, 512, 512, 1024


def setup_inputs():
    n = np.random.standard_normal
    s = mx_kscale(K)[:, None]
    u = mx_kscale(S)
    packed_xT = pack_weight(n((K, T)) * s)
    return {
        "x_words": packed_xT[0],
        "x_scales": packed_xT[1],
        "w1": (n((K, H)) / np.sqrt(K) / s).astype(np.float32),
        "w2": (n((K, H)) / np.sqrt(K) / s).astype(np.float32),
        "gk": (np.random.uniform(0.5, 1.5, (H, 1)) * u[:, None]).astype(np.float32),
        "gq": (np.random.uniform(0.5, 1.5, (H, 1)) / u[:, None]).astype(np.float32),
        "tab": n((S, U)).astype(np.float32),
        "wv": (n((K, N)) / np.sqrt(K) / s).astype(np.float32),
        "gi": (np.random.uniform(0.5, 1.5, (S, 1)) / u[:, None]).astype(np.float32),
        "gt": (np.random.uniform(0.5, 1.5, (S, 1)) * u[:, None]).astype(np.float32),
        "offs": striped(np.random.permutation(T)[:S]),
        "qs": striped(np.random.permutation(T)[:V]),
        "rel": striped8(np.random.randint(0, U, (8, V))),
    }


def reference(x_words, x_scales, w1, w2, gk, gq, tab, wv, gi, gt, offs, qs, rel):
    xq = unpack_weight(x_words, x_scales)[:, unstriped(offs)]
    val = xq.T @ mxq(f64(wv), 0, "e4m3")
    zv = f64(gi) * val
    kf = mxq(f64(w1), 0, "e4m3").T @ xq
    z = f64(gk) * kf
    x_qs = unpack_weight(x_words, x_scales)[:, unstriped(qs)]
    qf = mxq(f64(w2), 0, "e4m3").T @ x_qs
    z2 = f64(gq) * qf
    s = 0.0625 * ((mxq(z, 0, "e4m3").T @ mxq(z2, 0, "e4m3")))
    zp = f64(gt) * (sigmoid(s + f64(tab)[np.arange(S)[:, None], runs(rel, S)]))
    return 0.0625 * ((mxq(zv, 0, "e4m3").T @ mxq(zp, 0, "e4m3")))

@@ -1,0 +1,178 @@
+from contextlib import ExitStack
+
+import concourse.mybir as mybir
+
+K, T, S, V, N, H, U = 512, 2048, 512, 512, 512, 512, 1024
+FLOPS = 5 * 2 * 512 * 512 * 512
+
+F32 = mybir.dt.float32
+BF16 = mybir.dt.bfloat16
+I32 = mybir.dt.int32
+U32 = mybir.dt.uint32
+U16 = mybir.dt.uint16
+U8 = mybir.dt.uint8
+FP8X4 = mybir.dt.float8_e4m3fn_x4
+MULT = mybir.AluOpType.mult
+ADD = mybir.AluOpType.add
+COPY = mybir.ActivationFunctionType.Copy
+SIGMOID = mybir.ActivationFunctionType.Sigmoid
+
+P = 128
+PACK = 4
+W = 512
+CH = 128
+
+
+def tile_picked_listbias_sigmoid_p_kernel(tc, x_words, x_scales, w1, w2, gk, gq, tab, wv, gi, gt, offs, qs, rel, out):
+    nc = tc.nc
+    with ExitStack() as ctx:
+        lists = ctx.enter_context(tc.tile_pool(name="lists", bufs=1))
+        sb = ctx.enter_context(tc.tile_pool(name="sb", bufs=1))
+        psum = ctx.enter_context(tc.psum_pool(name="psum", bufs=1))
+
+        def tile(name, shape, dtype, tag=None):
+            return sb.tile(shape, dtype, name=name, tag=tag or name, align_bytes=64)
+
+        def bank(b, name):
+            return psum.tile([P, W], F32, name=name, tag="bank%d" % b)
+
+        def mx(name):
+            return tile(name + "_c", [P, W], U32), tile(name + "_s", [P, W], U8)
+
+        def quantize(dst, src, c0, c1):
+            nc.vector.quantize_mx(out=dst[0][:, c0:c1].bitcast(FP8X4), scales=dst[1][:, c0:c1], in_=src[:, PACK * c0 : PACK * c1])
+
+        def mm(o, lhs, l0, rhs, r0, n):
+            nc.tensor.matmul_mx(out=o, lhsT=lhs[0][:, l0 : l0 + P].bitcast(FP8X4), lhsT_scale=lhs[1][:, l0 : l0 + P],
+                                rhs=rhs[0][:, r0 : r0 + n].bitcast(FP8X4), rhs_scale=rhs[1][:, r0 : r0 + n], start=True, stop=True)
+
+        offs_t = lists.tile([P, S // 16], U16, name="offs_t")
+        qs_t = lists.tile([P, V // 16], U16, name="qs_t")
+        rel_t = lists.tile([P, V // 16], U16, name="rel_t")
+
+        xw = tile("xw", [P, T], I32)
+        xs = tile("xs", [P, T], U8)
+        warm = tile("warm", [P, 8], F32)
+        warm2 = tile("warm2", [P, 8], F32)
+
+        nc.vector.memset(xs[:].bitcast(I32), 0)
+        nc.vector.memset(warm[:], 0.0)
+        nc.sync.dma_start(qs_t[:], qs)
+        nc.sync.dma_start(out=xw[:], in_=x_words[0].rearrange("p c r -> p (c r)").bitcast(I32))
+        for q in range(4):
+            nc.scalar.dma_start(out=xs[32 * q : 32 * q + 4, :].bitcast(I32), in_=x_scales[0, 4 * q : 4 * q + 4, :].bitcast(I32))
+        nc.scalar.activation(warm2[:], warm[:], SIGMOID)
+        nc.sync.dma_start(offs_t[:], offs)
+
+        gains = {}
+        for name, g in (("gq", gq), ("gk", gk), ("gi", gi), ("gt", gt)):
+            gains[name] = tile(name + "_t", [P, PACK], F32)
+            nc.gpsimd.dma_start(out=gains[name][:], in_=g.rearrange("(p t) o -> p (t o)", t=PACK))
+
+        HW = W // 2
+        w2_raw = []
+        for h in range(2):
+            w2_raw.append(tile("w2_raw%d" % h, [P, PACK, HW], F32))
+            nc.sync.dma_start(out=w2_raw[h][:], in_=w2.rearrange("(p j) c -> p j c", j=PACK)[:, :, h * HW : (h + 1) * HW])
+        raw = {}
+        for name, w in (("w1", w1), ("wv", wv)):
+            raw[name] = tile(name + "_raw", [P, PACK, W], F32)
+            nc.sync.dma_start(out=raw[name][:], in_=w.rearrange("(p j) c -> p j c", j=PACK))
+        nc.sync.dma_start(rel_t[:], rel)
+        tabs = []
+        for t in range(PACK):
+            tabs.append(tile("tab%d" % t, [P, U], F32))
+            nc.sync.dma_start(out=tabs[t][:], in_=tab.rearrange("(p t) u -> p t u", t=PACK)[:, t, :])
+
+        def weigh(dst, src, gain):
+            nc.vector.tensor_tensor(dst.rearrange("p (n t) -> p n t", t=PACK), src, gain[:].unsqueeze(1).to_broadcast([P, CH, PACK]), MULT)
+
+        def weave(dst, src):
+            nc.scalar.copy(dst.rearrange("p (c i t) -> p c t i", i=4, t=PACK), src.rearrange("p t (c i) -> p c t i", i=4))
+
+        xk = mx("xk")
+        xq = mx("xq")
+        nc.vector.tensor_copy(xq[0][:], xw[:].bitcast(U32).indirect(qs_t[:]))
+        nc.vector.tensor_copy(xq[1][:], xs[:].indirect(qs_t[:]))
+        nc.vector.tensor_copy(xk[0][:].rearrange("p (t m) -> p m t", t=PACK), xw[:].bitcast(U32).indirect(offs_t[:]))
+
+        wb = {}
+        wq = {}
+        for name in ("w2", "w1", "wv"):
+            wb[name] = tile(name + "_b", [P, PACK * W], BF16)
+            wq[name] = mx(name)
+        for h in range(2):
+            nc.scalar.copy(wb["w2"][:].rearrange("p (t m j) -> p m j t", t=PACK, j=PACK)[:, h * 64 : (h + 1) * 64], w2_raw[h][:].rearrange("p j (m t) -> p m j t", t=PACK))
+        quantize(wq["w2"], wb["w2"], 0, W)
+        xk_plain = tile("xk_plain", [P, S], U8, tag="w2_b")
+        nc.vector.tensor_copy(xk_plain[:], xs[:].indirect(offs_t[:]))
+        nc.vector.tensor_copy(xk[1][:].rearrange("p (t m) -> p t m", t=PACK), xk_plain[:].rearrange("p (m t) -> p t m", t=PACK))
+        nc.scalar.copy(wb["w1"][:].rearrange("p (t m j) -> p m j t", t=PACK, j=PACK), raw["w1"][:].rearrange("p j (m t) -> p m j t", t=PACK))
+        quantize(wq["w1"], wb["w1"], 0, W)
+        nc.scalar.copy(wb["wv"][:].rearrange("p (c i j) -> p c j i", i=4, j=PACK), raw["wv"][:].rearrange("p j (c i) -> p c j i", i=4))
+
+        z2b = tile("z2b", [P, PACK * W], BF16)
+        z2q = mx("z2")
+        qb = [bank(4 + c, "qf%d" % c) for c in range(PACK)]
+        for c in range(PACK):
+            for t in range(PACK):
+                mm(qb[c][:, t * CH : (t + 1) * CH], wq["w2"], t * P, xq, c * CH, CH)
+            weigh(z2b[:, c * W : (c + 1) * W], qb[c][:].rearrange("p (t n) -> p n t", t=PACK), gains["gq"])
+
+        zplain = tile("zplain", [P, PACK, W], BF16)
+        kb = [bank(t, "kf%d" % t) for t in range(PACK)]
+        for t in range(PACK):
+            mm(kb[t][:], wq["w1"], t * P, xk, 0, W)
+            nc.scalar.activation(zplain[:, t, :], kb[t][:], COPY, scale=gains["gk"][:, t : t + 1])
+        zb = [tile("zb%d" % c, [P, W], BF16) for c in range(PACK)]
+        zq = [(tile("z_c%d" % c, [P, CH], U32), tile("z_s%d" % c, [P, CH], U8)) for c in range(PACK)]
+        for c in range(PACK):
+            weave(zb[c][:], zplain[:, :, c * CH : (c + 1) * CH])
+
+        bias = [tile("bias%d" % t, [P, V], F32) for t in range(PACK)]
+        quantize(z2q, z2b, 0, W)
+        quantize(wq["wv"], wb["wv"], 0, W)
+
+        NS = 3
+        zvb = tile("zvb", [P, PACK * W], BF16)
+        zvq = mx("zv")
+        vb = [bank(4 + c, "val%d" % c) for c in range(PACK)]
+        for c in range(PACK):
+            for t in range(PACK):
+                mm(vb[c][:, t * CH : (t + 1) * CH], xk, t * P, wq["wv"], c * CH, CH)
+            if c < NS:
+                vplain = tile("vplain%d" % c, [P, PACK, CH], BF16)
+                for t in range(PACK):
+                    nc.scalar.activation(vplain[:, t, :], vb[c][:, t * CH : (t + 1) * CH], COPY, scale=gains["gi"][:, t : t + 1])
+                weave(zvb[:, c * W : (c + 1) * W], vplain[:])
+
+        pre = tile("pre", [P, PACK, V], F32)
+        for t in range(PACK):
+            quantize(zq[t], zb[t], 0, CH)
+            nc.vector.tensor_copy(bias[t][:], tabs[t][:].indirect(rel_t[:]))
+            sbk = bank(t, "s%d" % t)
+            mm(sbk[:], zq[t], 0, z2q, 0, W)
+            nc.vector.scalar_tensor_tensor(pre[:, t, :], sbk[:], 0.0625, bias[t][:], MULT, ADD)
+
+        for c in range(NS, PACK):
+            weigh(zvb[:, c * W : (c + 1) * W], vb[c][:].rearrange("p (t n) -> p n t", t=PACK), gains["gi"])
+
+        sig = [tile("sig%d" % c, [P, W], F32) for c in range(PACK)]
+        for c in range(PACK):
+            nc.scalar.activation(sig[c][:].rearrange("p (n i t) -> p n t i", i=4, t=PACK),
+                                 pre[:, :, c * CH : (c + 1) * CH].rearrange("p t (n i) -> p n t i", i=4), SIGMOID)
+
+        zpb = [tile("zpb%d" % c, [P, W], BF16) for c in range(PACK)]
+        zpq = [(tile("zp_c%d" % c, [P, CH], U32), tile("zp_s%d" % c, [P, CH], U8)) for c in range(PACK)]
+        quantize(zvq, zvb, 0, W)
+        weigh(zpb[0][:], sig[0][:].rearrange("p (n t) -> p n t", t=PACK), gains["gt"])
+        for c in range(PACK):
+            if c + 1 < PACK:
+                weigh(zpb[c + 1][:], sig[c + 1][:].rearrange("p (n t) -> p n t", t=PACK), gains["gt"])
+            quantize(zpq[c], zpb[c], 0, CH)
+            ob = bank(c, "o%d" % c)
+            for a in range(PACK):
+                mm(ob[:, a * CH : (a + 1) * CH], zvq, a * P, zpq[c], 0, CH)
+            res = tile("res%d" % c, [P, W], F32)
+            nc.scalar.activation(res[:], ob[:], COPY, scale=0.0625)
+            nc.sync.dma_start(out=out.rearrange("(a p) v -> p a v", p=P)[:, :, c * CH : (c + 1) * CH], in_=res[:].rearrange("p (a n) -> p a n", a=PACK))

@@ -1,6 +1,7 @@
 from contextlib import ExitStack
 
 import concourse.mybir as mybir
+from concourse.masks import make_identity
 
 K, T, S, V, N, H, U = 512, 2048, 512, 512, 512, 512, 1024
 FLOPS = 5 * 2 * 512 * 512 * 512
@@ -21,6 +22,7 @@ P = 128
 PACK = 4
 W = 512
 CH = 128
+RUN = 8
 
 
 def tile_picked_listbias_sigmoid_p_kernel(tc, x_words, x_scales, w1, w2, gk, gq, tab, wv, gi, gt, offs, qs, rel, out):
@@ -56,24 +58,28 @@ def tile_picked_listbias_sigmoid_p_kernel(tc, x_words, x_scales, w1, w2, gk, gq,
         warm2 = tile("warm2", [P, 8], F32)
 
         nc.vector.memset(xs[:].bitcast(I32), 0)
-        nc.vector.memset(warm[:], 0.0)
+        nc.gpsimd.memset(warm[:], 0.0)
+        stage = tile("stage", [P, P], F32)
+        nc.gpsimd.memset(stage[:], 0.0)
+        ident = tile("ident", [P, P], F32)
+        make_identity(nc, ident[:])
         nc.sync.dma_start(qs_t[:], qs)
         nc.sync.dma_start(out=xw[:], in_=x_words[0].rearrange("p c r -> p (c r)").bitcast(I32))
-        for q in range(4):
-            nc.scalar.dma_start(out=xs[32 * q : 32 * q + 4, :].bitcast(I32), in_=x_scales[0, 4 * q : 4 * q + 4, :].bitcast(I32))
-        nc.scalar.activation(warm2[:], warm[:], SIGMOID)
         nc.sync.dma_start(offs_t[:], offs)
-
-        gains = {}
-        for name, g in (("gq", gq), ("gk", gk), ("gi", gi), ("gt", gt)):
-            gains[name] = tile(name + "_t", [P, PACK], F32)
-            nc.gpsimd.dma_start(out=gains[name][:], in_=g.rearrange("(p t) o -> p (t o)", t=PACK))
+        for q in range(4):
+            nc.sync.dma_start(out=xs[32 * q : 32 * q + 4, :].bitcast(I32), in_=x_scales[0, 4 * q : 4 * q + 4, :].bitcast(I32))
+        nc.scalar.activation(warm2[:], warm[:], SIGMOID)
 
         HW = W // 2
         w2_raw = []
         for h in range(2):
             w2_raw.append(tile("w2_raw%d" % h, [P, PACK, HW], F32))
             nc.sync.dma_start(out=w2_raw[h][:], in_=w2.rearrange("(p j) c -> p j c", j=PACK)[:, :, h * HW : (h + 1) * HW])
+        gain_t = tile("gain_t", [P, 4 * PACK], F32)
+        gains = {}
+        for r, (name, g) in enumerate((("gq", gq), ("gk", gk), ("gi", gi), ("gt", gt))):
+            nc.sync.dma_start(out=stage[PACK * r : PACK * (r + 1), :].rearrange("t (b e) -> t b e", e=RUN), in_=g.rearrange("(b t e) o -> t b (e o)", t=PACK, e=RUN))
+            gains[name] = gain_t[:, PACK * r : PACK * (r + 1)]
         raw = {}
         for name, w in (("w1", w1), ("wv", wv)):
             raw[name] = tile(name + "_raw", [P, PACK, W], F32)
@@ -82,10 +88,10 @@ def tile_picked_listbias_sigmoid_p_kernel(tc, x_words, x_scales, w1, w2, gk, gq,
         tabs = []
         for t in range(PACK):
             tabs.append(tile("tab%d" % t, [P, U], F32))
-            nc.sync.dma_start(out=tabs[t][:], in_=tab.rearrange("(p t) u -> p t u", t=PACK)[:, t, :])
+            nc.sync.dma_start(out=tabs[t][:], in_=tab.rearrange("(b t e) u -> t b e u", t=PACK, e=RUN)[t])
 
         def weigh(dst, src, gain):
-            nc.vector.tensor_tensor(dst.rearrange("p (n t) -> p n t", t=PACK), src, gain[:].unsqueeze(1).to_broadcast([P, CH, PACK]), MULT)
+            nc.vector.tensor_tensor(dst.rearrange("p (n t) -> p n t", t=PACK), src, gain.unsqueeze(1).to_broadcast([P, CH, PACK]), MULT)
 
         def weave(dst, src):
             nc.scalar.copy(dst.rearrange("p (c i t) -> p c t i", i=4, t=PACK), src.rearrange("p t (c i) -> p c t i", i=4))
@@ -94,20 +100,29 @@ def tile_picked_listbias_sigmoid_p_kernel(tc, x_words, x_scales, w1, w2, gk, gq,
         xq = mx("xq")
         nc.vector.tensor_copy(xq[0][:], xw[:].bitcast(U32).indirect(qs_t[:]))
         nc.vector.tensor_copy(xq[1][:], xs[:].indirect(qs_t[:]))
-        nc.vector.tensor_copy(xk[0][:].rearrange("p (t m) -> p m t", t=PACK), xw[:].bitcast(U32).indirect(offs_t[:]))
+        nc.vector.tensor_copy(xk[0][:].rearrange("p (t b e) -> p b t e", t=PACK, e=RUN), xw[:].bitcast(U32).indirect(offs_t[:]))
 
         wb = {}
         wq = {}
         for name in ("w2", "w1", "wv"):
             wb[name] = tile(name + "_b", [P, PACK * W], BF16)
             wq[name] = mx(name)
+        def deal(dst, src, t):
+            nc.scalar.copy(dst.rearrange("p (b f i j) -> p b f j i", f=2, i=4, j=PACK),
+                           src.rearrange("p j (b t f i) -> p t b f j i", t=PACK, f=2, i=4)[:, t])
+
         for h in range(2):
-            nc.scalar.copy(wb["w2"][:].rearrange("p (t m j) -> p m j t", t=PACK, j=PACK)[:, h * 64 : (h + 1) * 64], w2_raw[h][:].rearrange("p j (m t) -> p m j t", t=PACK))
+            for t in range(PACK):
+                deal(wb["w2"][:, t * W + h * HW : t * W + (h + 1) * HW], w2_raw[h][:], t)
+        turned = bank(0, "turned")
+        nc.tensor.transpose(turned[:, 0:P], stage[:], ident[:])
+        nc.scalar.copy(gain_t[:], turned[:, 0 : 4 * PACK])
         quantize(wq["w2"], wb["w2"], 0, W)
         xk_plain = tile("xk_plain", [P, S], U8, tag="w2_b")
         nc.vector.tensor_copy(xk_plain[:], xs[:].indirect(offs_t[:]))
-        nc.vector.tensor_copy(xk[1][:].rearrange("p (t m) -> p t m", t=PACK), xk_plain[:].rearrange("p (m t) -> p t m", t=PACK))
-        nc.scalar.copy(wb["w1"][:].rearrange("p (t m j) -> p m j t", t=PACK, j=PACK), raw["w1"][:].rearrange("p j (m t) -> p m j t", t=PACK))
+        nc.vector.tensor_copy(xk[1][:].bitcast(I32).rearrange("p (t b w) -> p t b w", t=PACK, w=2), xk_plain[:].bitcast(I32).rearrange("p (b t w) -> p t b w", t=PACK, w=2))
+        for t in range(PACK):
+            deal(wb["w1"][:, t * W : (t + 1) * W], raw["w1"][:], t)
         quantize(wq["w1"], wb["w1"], 0, W)
         nc.scalar.copy(wb["wv"][:].rearrange("p (c i j) -> p c j i", i=4, j=PACK), raw["wv"][:].rearrange("p j (c i) -> p c j i", i=4))
 
@@ -170,9 +185,23 @@ def tile_picked_listbias_sigmoid_p_kernel(tc, x_words, x_scales, w1, w2, gk, gq,
             if c + 1 < PACK:
                 weigh(zpb[c + 1][:], sig[c + 1][:].rearrange("p (n t) -> p n t", t=PACK), gains["gt"])
             quantize(zpq[c], zpb[c], 0, CH)
-            ob = bank(c, "o%d" % c)
-            for a in range(PACK):
-                mm(ob[:, a * CH : (a + 1) * CH], zvq, a * P, zpq[c], 0, CH)
-            res = tile("res%d" % c, [P, W], F32)
-            nc.scalar.activation(res[:], ob[:], COPY, scale=0.0625)
-            nc.sync.dma_start(out=out.rearrange("(a p) v -> p a v", p=P)[:, :, c * CH : (c + 1) * CH], in_=res[:].rearrange("p (a n) -> p a n", a=PACK))
+            rows = out.rearrange("(a p) v -> p a v", p=P)[:, :, c * CH : (c + 1) * CH]
+            if c + 1 < PACK:
+                ob = bank(c, "o%d" % c)
+                for a in range(PACK):
+                    mm(ob[:, a * CH : (a + 1) * CH], zvq, a * P, zpq[c], 0, CH)
+                res = tile("res%d" % c, [P, W], F32)
+                nc.scalar.activation(res[:], ob[:], COPY, scale=0.0625)
+                nc.sync.dma_start(out=rows, in_=res[:].rearrange("p (a n) -> p a n", a=PACK))
+            else:
+                for h in range(2):
+                    ob = bank(c + 4 * h, "o%d_%d" % (c, h))
+                    for a in range(2):
+                        mm(ob[:, a * CH : (a + 1) * CH], zvq, (2 * h + a) * P, zpq[c], 0, CH)
+                    res = tile("res%d_%d" % (c, h), [P, 2 * CH], F32)
+                    if h == 0:
+                        nc.scalar.activation(res[:], ob[:, 0 : 2 * CH], COPY, scale=0.0625)
+                        nc.scalar.dma_start(out=rows[:, 0:2], in_=res[:].rearrange("p (a n) -> p a n", a=2))
+                    else:
+                        nc.vector.tensor_scalar(res[:], ob[:, 0 : 2 * CH], 0.0625, None, MULT)
+                        nc.sync.dma_start(out=rows[:, 2:4], in_=res[:].rearrange("p (a n) -> p a n", a=2))

@@ -59,15 +59,21 @@ def tile_picked_listbias_sigmoid_p_kernel(tc, x_words, x_scales, w1, w2, gk, gq,
 
         nc.vector.memset(xs[:].bitcast(I32), 0)
         nc.gpsimd.memset(warm[:], 0.0)
-        stage = tile("stage", [P, P], F32)
+        stage = tile("stage", [P, W], F32)
+        rows4 = tile("rows4", [4, W], F32)
         nc.gpsimd.memset(stage[:], 0.0)
         ident = tile("ident", [P, P], F32)
         make_identity(nc, ident[:])
         nc.sync.dma_start(qs_t[:], qs)
-        nc.sync.dma_start(out=xw[:], in_=x_words[0].rearrange("p c r -> p (c r)").bitcast(I32))
         nc.sync.dma_start(offs_t[:], offs)
+        nc.sync.dma_start(out=xw[:], in_=x_words[0].rearrange("p c r -> p (c r)").bitcast(I32))
         for q in range(4):
-            nc.sync.dma_start(out=xs[32 * q : 32 * q + 4, :].bitcast(I32), in_=x_scales[0, 4 * q : 4 * q + 4, :].bitcast(I32))
+            nc.scalar.dma_start(out=xs[q:P:32, :].bitcast(I32), in_=x_scales[0, q:16:4, :].bitcast(I32))
+        gain_t = tile("gain_t", [P, 4 * PACK], F32)
+        gains = {}
+        for r, (name, g) in enumerate((("gq", gq), ("gk", gk), ("gi", gi), ("gt", gt))):
+            nc.scalar.dma_start(out=rows4[r : r + 1, :], in_=g.rearrange("c o -> o c"))
+            gains[name] = gain_t[:, PACK * r : PACK * (r + 1)]
         nc.scalar.activation(warm2[:], warm[:], SIGMOID)
 
         HW = W // 2
@@ -75,11 +81,6 @@ def tile_picked_listbias_sigmoid_p_kernel(tc, x_words, x_scales, w1, w2, gk, gq,
         for h in range(2):
             w2_raw.append(tile("w2_raw%d" % h, [P, PACK, HW], F32))
             nc.sync.dma_start(out=w2_raw[h][:], in_=w2.rearrange("(p j) c -> p j c", j=PACK)[:, :, h * HW : (h + 1) * HW])
-        gain_t = tile("gain_t", [P, 4 * PACK], F32)
-        gains = {}
-        for r, (name, g) in enumerate((("gq", gq), ("gk", gk), ("gi", gi), ("gt", gt))):
-            nc.sync.dma_start(out=stage[PACK * r : PACK * (r + 1), :].rearrange("t (b e) -> t b e", e=RUN), in_=g.rearrange("(b t e) o -> t b (e o)", t=PACK, e=RUN))
-            gains[name] = gain_t[:, PACK * r : PACK * (r + 1)]
         raw = {}
         for name, w in (("w1", w1), ("wv", wv)):
             raw[name] = tile(name + "_raw", [P, PACK, W], F32)
@@ -107,16 +108,19 @@ def tile_picked_listbias_sigmoid_p_kernel(tc, x_words, x_scales, w1, w2, gk, gq,
         for name in ("w2", "w1", "wv"):
             wb[name] = tile(name + "_b", [P, PACK * W], BF16)
             wq[name] = mx(name)
+        turned = bank(0, "turned")
+        nc.scalar.copy(stage[0:4, :].rearrange("r (t b e) -> r t b e", t=PACK, e=RUN), rows4[:].rearrange("r (b t e) -> r t b e", t=PACK, e=RUN))
+        for t in range(PACK):
+            nc.tensor.transpose(turned[:, t * P : (t + 1) * P], stage[:, t * P : (t + 1) * P], ident[:])
+        nc.scalar.copy(gain_t[:].rearrange("p (r t) -> p r t", t=PACK), turned[:].rearrange("p (t r) -> p r t", t=PACK)[:, 0:4, :])
+
         def deal(dst, src, t):
-            nc.scalar.copy(dst.rearrange("p (b f i j) -> p b f j i", f=2, i=4, j=PACK),
-                           src.rearrange("p j (b t f i) -> p t b f j i", t=PACK, f=2, i=4)[:, t])
+            nc.scalar.copy(dst.rearrange("p (b f i j) -> p b f j i", f=4, i=2, j=PACK),
+                           src.rearrange("p j (b t f i) -> p t b f j i", t=PACK, f=4, i=2)[:, t])
 
         for h in range(2):
             for t in range(PACK):
                 deal(wb["w2"][:, t * W + h * HW : t * W + (h + 1) * HW], w2_raw[h][:], t)
-        turned = bank(0, "turned")
-        nc.tensor.transpose(turned[:, 0:P], stage[:], ident[:])
-        nc.scalar.copy(gain_t[:], turned[:, 0 : 4 * PACK])
         quantize(wq["w2"], wb["w2"], 0, W)
         xk_plain = tile("xk_plain", [P, S], U8, tag="w2_b")
         nc.vector.tensor_copy(xk_plain[:], xs[:].indirect(offs_t[:]))
@@ -124,15 +128,15 @@ def tile_picked_listbias_sigmoid_p_kernel(tc, x_words, x_scales, w1, w2, gk, gq,
         for t in range(PACK):
             deal(wb["w1"][:, t * W : (t + 1) * W], raw["w1"][:], t)
         quantize(wq["w1"], wb["w1"], 0, W)
-        nc.scalar.copy(wb["wv"][:].rearrange("p (c i j) -> p c j i", i=4, j=PACK), raw["wv"][:].rearrange("p j (c i) -> p c j i", i=4))
+        nc.scalar.copy(wb["wv"][:].rearrange("p (c i j) -> p c j i", i=2, j=PACK), raw["wv"][:].rearrange("p j (c i) -> p c j i", i=2))
 
-        z2b = tile("z2b", [P, PACK * W], BF16)
+        z2b = [tile("z2b0", [P, 2 * W], BF16), tile("z2b1", [P, 2 * W], BF16, tag="w1_b")]
         z2q = mx("z2")
         qb = [bank(4 + c, "qf%d" % c) for c in range(PACK)]
         for c in range(PACK):
             for t in range(PACK):
                 mm(qb[c][:, t * CH : (t + 1) * CH], wq["w2"], t * P, xq, c * CH, CH)
-            weigh(z2b[:, c * W : (c + 1) * W], qb[c][:].rearrange("p (t n) -> p n t", t=PACK), gains["gq"])
+            weigh(z2b[c // 2][:, c % 2 * W : (c % 2 + 1) * W], qb[c][:].rearrange("p (t n) -> p n t", t=PACK), gains["gq"])
 
         zplain = tile("zplain", [P, PACK, W], BF16)
         kb = [bank(t, "kf%d" % t) for t in range(PACK)]
@@ -145,37 +149,44 @@ def tile_picked_listbias_sigmoid_p_kernel(tc, x_words, x_scales, w1, w2, gk, gq,
             weave(zb[c][:], zplain[:, :, c * CH : (c + 1) * CH])
 
         bias = [tile("bias%d" % t, [P, V], F32) for t in range(PACK)]
-        quantize(z2q, z2b, 0, W)
+        for h in range(2):
+            nc.vector.quantize_mx(out=z2q[0][:, h * HW : (h + 1) * HW].bitcast(FP8X4), scales=z2q[1][:, h * HW : (h + 1) * HW], in_=z2b[h][:])
         quantize(wq["wv"], wb["wv"], 0, W)
 
         NS = 3
         zvb = tile("zvb", [P, PACK * W], BF16)
         zvq = mx("zv")
         vb = [bank(4 + c, "val%d" % c) for c in range(PACK)]
-        for c in range(PACK):
+        vplain = tile("vplain", [P, PACK, NS * CH], BF16)
+        for t in range(PACK):
+            mm(vb[t // 2][:, t % 2 * HW : (t % 2 + 1) * HW], xk, t * P, wq["wv"], 0, HW)
+        for c in range(2, PACK):
             for t in range(PACK):
                 mm(vb[c][:, t * CH : (t + 1) * CH], xk, t * P, wq["wv"], c * CH, CH)
-            if c < NS:
-                vplain = tile("vplain%d" % c, [P, PACK, CH], BF16)
-                for t in range(PACK):
-                    nc.scalar.activation(vplain[:, t, :], vb[c][:, t * CH : (t + 1) * CH], COPY, scale=gains["gi"][:, t : t + 1])
-                weave(zvb[:, c * W : (c + 1) * W], vplain[:])
-
-        pre = tile("pre", [P, PACK, V], F32)
         for t in range(PACK):
-            quantize(zq[t], zb[t], 0, CH)
-            nc.vector.tensor_copy(bias[t][:], tabs[t][:].indirect(rel_t[:]))
-            sbk = bank(t, "s%d" % t)
-            mm(sbk[:], zq[t], 0, z2q, 0, W)
-            nc.vector.scalar_tensor_tensor(pre[:, t, :], sbk[:], 0.0625, bias[t][:], MULT, ADD)
+            nc.scalar.activation(vplain[:, t, 0:HW], vb[t // 2][:, t % 2 * HW : (t % 2 + 1) * HW], COPY, scale=gains["gi"][:, t : t + 1])
+        for t in range(PACK):
+            nc.scalar.activation(vplain[:, t, HW : HW + CH], vb[2][:, t * CH : (t + 1) * CH], COPY, scale=gains["gi"][:, t : t + 1])
+        weave(zvb[:, 0 : NS * W], vplain[:])
 
         for c in range(NS, PACK):
             weigh(zvb[:, c * W : (c + 1) * W], vb[c][:].rearrange("p (t n) -> p n t", t=PACK), gains["gi"])
 
+        pre = tile("pre", [P, PACK, V], F32)
+        for t in range(PACK):
+            quantize(zq[t], zb[t], 0, CH)
+            sbk = bank(t, "s%d" % t)
+            mm(sbk[:], zq[t], 0, z2q, 0, W)
+            pieces = 2 if t == PACK - 1 else 1
+            for h in range(pieces):
+                n = V // pieces
+                nc.vector.tensor_copy(bias[t][:, h * n : (h + 1) * n], tabs[t][:].indirect(rel_t[:, h * n // 16 : (h + 1) * n // 16]))
+                nc.vector.scalar_tensor_tensor(pre[:, t, h * n : (h + 1) * n], sbk[:, h * n : (h + 1) * n], 0.0625, bias[t][:, h * n : (h + 1) * n], MULT, ADD)
+
         sig = [tile("sig%d" % c, [P, W], F32) for c in range(PACK)]
         for c in range(PACK):
-            nc.scalar.activation(sig[c][:].rearrange("p (n i t) -> p n t i", i=4, t=PACK),
-                                 pre[:, :, c * CH : (c + 1) * CH].rearrange("p t (n i) -> p n t i", i=4), SIGMOID)
+            nc.scalar.activation(sig[c][:].rearrange("p (n i t) -> p n t i", i=2, t=PACK),
+                                 pre[:, :, c * CH : (c + 1) * CH].rearrange("p t (n i) -> p n t i", i=2), SIGMOID)
 
         zpb = [tile("zpb%d" % c, [P, W], BF16) for c in range(PACK)]
         zpq = [(tile("zp_c%d" % c, [P, CH], U32), tile("zp_s%d" % c, [P, CH], U8)) for c in range(PACK)]

@@ -1,9 +1,8 @@
 from contextlib import ExitStack
 
 import concourse.mybir as mybir
-from concourse.masks import make_identity
 
-K, T, S, V, N, H, U = 512, 2048, 512, 512, 512, 512, 1024
+T, U = 2048, 1024
 FLOPS = 5 * 2 * 512 * 512 * 512
 
 F32 = mybir.dt.float32
@@ -21,8 +20,9 @@ SIGMOID = mybir.ActivationFunctionType.Sigmoid
 P = 128
 PACK = 4
 W = 512
+HW = W // 2
 CH = 128
-RUN = 8
+SIXTEENTH = 0.0625
 
 
 def tile_picked_listbias_sigmoid_p_kernel(tc, x_words, x_scales, w1, w2, gk, gq, tab, wv, gi, gt, offs, qs, rel, out):
@@ -38,45 +38,47 @@ def tile_picked_listbias_sigmoid_p_kernel(tc, x_words, x_scales, w1, w2, gk, gq,
         def bank(b, name):
             return psum.tile([P, W], F32, name=name, tag="bank%d" % b)
 
-        def mx(name):
-            return tile(name + "_c", [P, W], U32), tile(name + "_s", [P, W], U8)
+        def mx(name, width=W):
+            return tile(name + "_c", [P, width], U32), tile(name + "_s", [P, width], U8)
 
-        def quantize(dst, src, c0, c1):
-            nc.vector.quantize_mx(out=dst[0][:, c0:c1].bitcast(FP8X4), scales=dst[1][:, c0:c1], in_=src[:, PACK * c0 : PACK * c1])
+        def quantize(dst, c0, src):
+            c1 = c0 + src.shape[1] // PACK
+            nc.vector.quantize_mx(out=dst[0][:, c0:c1].bitcast(FP8X4), scales=dst[1][:, c0:c1], in_=src)
 
         def mm(o, lhs, l0, rhs, r0, n):
             nc.tensor.matmul_mx(out=o, lhsT=lhs[0][:, l0 : l0 + P].bitcast(FP8X4), lhsT_scale=lhs[1][:, l0 : l0 + P],
                                 rhs=rhs[0][:, r0 : r0 + n].bitcast(FP8X4), rhs_scale=rhs[1][:, r0 : r0 + n], start=True, stop=True)
 
-        offs_t = lists.tile([P, S // 16], U16, name="offs_t")
-        qs_t = lists.tile([P, V // 16], U16, name="qs_t")
-        rel_t = lists.tile([P, V // 16], U16, name="rel_t")
+        def deal(dst, src):
+            nc.scalar.copy(dst, src.rearrange("p j (m t) -> p m j t", t=PACK))
+
+        def dealt(whole):
+            return whole[:].rearrange("p (t m j) -> p m j t", t=PACK, j=PACK)
+
+        def weigh(dst, src, gain):
+            nc.vector.tensor_tensor(dst.rearrange("p (n t) -> p n t", t=PACK), src, gain[:].unsqueeze(1).to_broadcast([P, CH, PACK]), MULT)
+
+        def weave(dst, src):
+            nc.scalar.copy(dst.rearrange("p (c t) -> p c t", t=PACK), src.rearrange("p t c -> p c t"))
+
+        offs_t = lists.tile([P, W // 16], U16, name="offs_t")
+        qs_t = lists.tile([P, W // 16], U16, name="qs_t")
+        rel_t = lists.tile([P, W // 16], U16, name="rel_t")
 
         xw = tile("xw", [P, T], I32)
         xs = tile("xs", [P, T], U8)
-        warm = tile("warm", [P, 8], F32)
-        warm2 = tile("warm2", [P, 8], F32)
-
         nc.vector.memset(xs[:].bitcast(I32), 0)
-        nc.gpsimd.memset(warm[:], 0.0)
-        stage = tile("stage", [P, W], F32)
-        rows4 = tile("rows4", [4, W], F32)
-        nc.gpsimd.memset(stage[:], 0.0)
-        ident = tile("ident", [P, P], F32)
-        make_identity(nc, ident[:])
         nc.sync.dma_start(qs_t[:], qs)
-        nc.sync.dma_start(offs_t[:], offs)
         nc.sync.dma_start(out=xw[:], in_=x_words[0].rearrange("p c r -> p (c r)").bitcast(I32))
-        for q in range(4):
-            nc.scalar.dma_start(out=xs[q:P:32, :].bitcast(I32), in_=x_scales[0, q:16:4, :].bitcast(I32))
-        gain_t = tile("gain_t", [P, 4 * PACK], F32)
-        gains = {}
-        for r, (name, g) in enumerate((("gq", gq), ("gk", gk), ("gi", gi), ("gt", gt))):
-            nc.scalar.dma_start(out=rows4[r : r + 1, :], in_=g.rearrange("c o -> o c"))
-            gains[name] = gain_t[:, PACK * r : PACK * (r + 1)]
-        nc.scalar.activation(warm2[:], warm[:], SIGMOID)
+        for r in range(4):
+            nc.scalar.dma_start(out=xs[r:P:32, :].bitcast(I32), in_=x_scales[0, r:16:4, :].bitcast(I32))
+        nc.sync.dma_start(offs_t[:], offs)
 
-        HW = W // 2
+        gains = {}
+        for name, g in (("gq", gq), ("gk", gk), ("gi", gi), ("gt", gt)):
+            gains[name] = tile(name + "_t", [P, PACK], F32)
+            nc.gpsimd.dma_start(out=gains[name][:], in_=g.rearrange("(p t) o -> p (t o)", t=PACK))
+
         w2_raw = []
         for h in range(2):
             w2_raw.append(tile("w2_raw%d" % h, [P, PACK, HW], F32))
@@ -89,75 +91,55 @@ def tile_picked_listbias_sigmoid_p_kernel(tc, x_words, x_scales, w1, w2, gk, gq,
         tabs = []
         for t in range(PACK):
             tabs.append(tile("tab%d" % t, [P, U], F32))
-            nc.sync.dma_start(out=tabs[t][:], in_=tab.rearrange("(b t e) u -> t b e u", t=PACK, e=RUN)[t])
-
-        def weigh(dst, src, gain):
-            nc.vector.tensor_tensor(dst.rearrange("p (n t) -> p n t", t=PACK), src, gain.unsqueeze(1).to_broadcast([P, CH, PACK]), MULT)
-
-        def weave(dst, src):
-            nc.scalar.copy(dst.rearrange("p (c i t) -> p c t i", i=4, t=PACK), src.rearrange("p t (c i) -> p c t i", i=4))
+            nc.sync.dma_start(out=tabs[t][:], in_=tab.rearrange("(p t) u -> p t u", t=PACK)[:, t, :])
 
         xk = mx("xk")
         xq = mx("xq")
         nc.vector.tensor_copy(xq[0][:], xw[:].bitcast(U32).indirect(qs_t[:]))
         nc.vector.tensor_copy(xq[1][:], xs[:].indirect(qs_t[:]))
-        nc.vector.tensor_copy(xk[0][:].rearrange("p (t b e) -> p b t e", t=PACK, e=RUN), xw[:].bitcast(U32).indirect(offs_t[:]))
+        nc.vector.tensor_copy(xk[0][:].rearrange("p (t m) -> p m t", t=PACK), xw[:].bitcast(U32).indirect(offs_t[:]))
 
         wb = {}
         wq = {}
         for name in ("w2", "w1", "wv"):
             wb[name] = tile(name + "_b", [P, PACK * W], BF16)
             wq[name] = mx(name)
-        turned = bank(0, "turned")
-        nc.scalar.copy(stage[0:4, :].rearrange("r (t b e) -> r t b e", t=PACK, e=RUN), rows4[:].rearrange("r (b t e) -> r t b e", t=PACK, e=RUN))
-        for t in range(PACK):
-            nc.tensor.transpose(turned[:, t * P : (t + 1) * P], stage[:, t * P : (t + 1) * P], ident[:])
-        nc.scalar.copy(gain_t[:].rearrange("p (r t) -> p r t", t=PACK), turned[:].rearrange("p (t r) -> p r t", t=PACK)[:, 0:4, :])
-
-        def deal(dst, src, t):
-            nc.scalar.copy(dst.rearrange("p (b f i j) -> p b f j i", f=4, i=2, j=PACK),
-                           src.rearrange("p j (b t f i) -> p t b f j i", t=PACK, f=4, i=2)[:, t])
-
         for h in range(2):
-            for t in range(PACK):
-                deal(wb["w2"][:, t * W + h * HW : t * W + (h + 1) * HW], w2_raw[h][:], t)
-        quantize(wq["w2"], wb["w2"], 0, W)
-        xk_plain = tile("xk_plain", [P, S], U8, tag="w2_b")
+            deal(dealt(wb["w2"])[:, h * 64 : (h + 1) * 64], w2_raw[h][:])
+        quantize(wq["w2"], 0, wb["w2"][:])
+        xk_plain = tile("xk_plain", [P, W], U8, tag="w2_b")
         nc.vector.tensor_copy(xk_plain[:], xs[:].indirect(offs_t[:]))
-        nc.vector.tensor_copy(xk[1][:].bitcast(I32).rearrange("p (t b w) -> p t b w", t=PACK, w=2), xk_plain[:].bitcast(I32).rearrange("p (b t w) -> p t b w", t=PACK, w=2))
-        for t in range(PACK):
-            deal(wb["w1"][:, t * W : (t + 1) * W], raw["w1"][:], t)
-        quantize(wq["w1"], wb["w1"], 0, W)
-        nc.scalar.copy(wb["wv"][:].rearrange("p (c i j) -> p c j i", i=2, j=PACK), raw["wv"][:].rearrange("p j (c i) -> p c j i", i=2))
+        nc.vector.tensor_copy(xk[1][:].rearrange("p (t m) -> p t m", t=PACK), xk_plain[:].rearrange("p (m t) -> p t m", t=PACK))
+        deal(dealt(wb["w1"]), raw["w1"][:])
+        quantize(wq["w1"], 0, wb["w1"][:])
+        deal(dealt(wb["wv"]), raw["wv"][:])
 
         z2b = [tile("z2b0", [P, 2 * W], BF16), tile("z2b1", [P, 2 * W], BF16, tag="w1_b")]
         z2q = mx("z2")
-        qb = [bank(4 + c, "qf%d" % c) for c in range(PACK)]
         for c in range(PACK):
+            qb = bank(4 + c, "qf%d" % c)
             for t in range(PACK):
-                mm(qb[c][:, t * CH : (t + 1) * CH], wq["w2"], t * P, xq, c * CH, CH)
-            weigh(z2b[c // 2][:, c % 2 * W : (c % 2 + 1) * W], qb[c][:].rearrange("p (t n) -> p n t", t=PACK), gains["gq"])
+                mm(qb[:, t * CH : (t + 1) * CH], wq["w2"], t * P, xq, c * CH, CH)
+            weigh(z2b[c // 2][:, c % 2 * W : (c % 2 + 1) * W], qb[:].rearrange("p (t n) -> p n t", t=PACK), gains["gq"])
 
         zplain = tile("zplain", [P, PACK, W], BF16)
-        kb = [bank(t, "kf%d" % t) for t in range(PACK)]
         for t in range(PACK):
-            mm(kb[t][:], wq["w1"], t * P, xk, 0, W)
-            nc.scalar.activation(zplain[:, t, :], kb[t][:], COPY, scale=gains["gk"][:, t : t + 1])
+            kb = bank(t, "kf%d" % t)
+            mm(kb[:], wq["w1"], t * P, xk, 0, W)
+            nc.scalar.activation(zplain[:, t, :], kb[:], COPY, scale=gains["gk"][:, t : t + 1])
         zb = [tile("zb%d" % c, [P, W], BF16) for c in range(PACK)]
-        zq = [(tile("z_c%d" % c, [P, CH], U32), tile("z_s%d" % c, [P, CH], U8)) for c in range(PACK)]
+        zq = [mx("z%d_" % c, CH) for c in range(PACK)]
         for c in range(PACK):
             weave(zb[c][:], zplain[:, :, c * CH : (c + 1) * CH])
 
-        bias = [tile("bias%d" % t, [P, V], F32) for t in range(PACK)]
         for h in range(2):
-            nc.vector.quantize_mx(out=z2q[0][:, h * HW : (h + 1) * HW].bitcast(FP8X4), scales=z2q[1][:, h * HW : (h + 1) * HW], in_=z2b[h][:])
-        quantize(wq["wv"], wb["wv"], 0, W)
+            quantize(z2q, h * HW, z2b[h][:])
+        quantize(wq["wv"], 0, wb["wv"][:])
 
-        NS = 3
         zvb = tile("zvb", [P, PACK * W], BF16)
         zvq = mx("zv")
         vb = [bank(4 + c, "val%d" % c) for c in range(PACK)]
-        vplain = tile("vplain", [P, PACK, NS * CH], BF16)
+        vplain = tile("vplain", [P, PACK, 3 * CH], BF16)
         for t in range(PACK):
             mm(vb[t // 2][:, t % 2 * HW : (t % 2 + 1) * HW], xk, t * P, wq["wv"], 0, HW)
         for c in range(2, PACK):
@@ -167,52 +149,51 @@ def tile_picked_listbias_sigmoid_p_kernel(tc, x_words, x_scales, w1, w2, gk, gq,
             nc.scalar.activation(vplain[:, t, 0:HW], vb[t // 2][:, t % 2 * HW : (t % 2 + 1) * HW], COPY, scale=gains["gi"][:, t : t + 1])
         for t in range(PACK):
             nc.scalar.activation(vplain[:, t, HW : HW + CH], vb[2][:, t * CH : (t + 1) * CH], COPY, scale=gains["gi"][:, t : t + 1])
-        weave(zvb[:, 0 : NS * W], vplain[:])
+        weave(zvb[:, 0 : 3 * W], vplain[:])
+        weigh(zvb[:, 3 * W : 4 * W], vb[3][:].rearrange("p (t n) -> p n t", t=PACK), gains["gi"])
 
-        for c in range(NS, PACK):
-            weigh(zvb[:, c * W : (c + 1) * W], vb[c][:].rearrange("p (t n) -> p n t", t=PACK), gains["gi"])
-
-        pre = tile("pre", [P, PACK, V], F32)
+        bias = [tile("bias%d" % t, [P, W], F32) for t in range(PACK)]
+        pre = tile("pre", [P, PACK, W], F32)
         for t in range(PACK):
-            quantize(zq[t], zb[t], 0, CH)
+            quantize(zq[t], 0, zb[t][:])
             sbk = bank(t, "s%d" % t)
             mm(sbk[:], zq[t], 0, z2q, 0, W)
             pieces = 2 if t == PACK - 1 else 1
+            n = W // pieces
             for h in range(pieces):
-                n = V // pieces
                 nc.vector.tensor_copy(bias[t][:, h * n : (h + 1) * n], tabs[t][:].indirect(rel_t[:, h * n // 16 : (h + 1) * n // 16]))
-                nc.vector.scalar_tensor_tensor(pre[:, t, h * n : (h + 1) * n], sbk[:, h * n : (h + 1) * n], 0.0625, bias[t][:, h * n : (h + 1) * n], MULT, ADD)
+                nc.vector.scalar_tensor_tensor(pre[:, t, h * n : (h + 1) * n], sbk[:, h * n : (h + 1) * n], SIXTEENTH, bias[t][:, h * n : (h + 1) * n], MULT, ADD)
 
         sig = [tile("sig%d" % c, [P, W], F32) for c in range(PACK)]
         for c in range(PACK):
-            nc.scalar.activation(sig[c][:].rearrange("p (n i t) -> p n t i", i=2, t=PACK),
-                                 pre[:, :, c * CH : (c + 1) * CH].rearrange("p t (n i) -> p n t i", i=2), SIGMOID)
+            nc.scalar.activation(sig[c][:].rearrange("p (n i t) -> p n t i", i=4, t=PACK),
+                                 pre[:, :, c * CH : (c + 1) * CH].rearrange("p t (n i) -> p n t i", i=4), SIGMOID)
 
         zpb = [tile("zpb%d" % c, [P, W], BF16) for c in range(PACK)]
-        zpq = [(tile("zp_c%d" % c, [P, CH], U32), tile("zp_s%d" % c, [P, CH], U8)) for c in range(PACK)]
-        quantize(zvq, zvb, 0, W)
+        zpq = [mx("zp%d_" % c, CH) for c in range(PACK)]
+        quantize(zvq, 0, zvb[:])
         weigh(zpb[0][:], sig[0][:].rearrange("p (n t) -> p n t", t=PACK), gains["gt"])
         for c in range(PACK):
             if c + 1 < PACK:
                 weigh(zpb[c + 1][:], sig[c + 1][:].rearrange("p (n t) -> p n t", t=PACK), gains["gt"])
-            quantize(zpq[c], zpb[c], 0, CH)
-            rows = out.rearrange("(a p) v -> p a v", p=P)[:, :, c * CH : (c + 1) * CH]
+            quantize(zpq[c], 0, zpb[c][:])
+            rows = out.rearrange("(p a) v -> p a v", a=PACK)[:, :, c * CH : (c + 1) * CH]
             if c + 1 < PACK:
                 ob = bank(c, "o%d" % c)
                 for a in range(PACK):
                     mm(ob[:, a * CH : (a + 1) * CH], zvq, a * P, zpq[c], 0, CH)
                 res = tile("res%d" % c, [P, W], F32)
-                nc.scalar.activation(res[:], ob[:], COPY, scale=0.0625)
+                nc.scalar.activation(res[:], ob[:], COPY, scale=SIXTEENTH)
                 nc.sync.dma_start(out=rows, in_=res[:].rearrange("p (a n) -> p a n", a=PACK))
             else:
                 for h in range(2):
                     ob = bank(c + 4 * h, "o%d_%d" % (c, h))
                     for a in range(2):
                         mm(ob[:, a * CH : (a + 1) * CH], zvq, (2 * h + a) * P, zpq[c], 0, CH)
-                    res = tile("res%d_%d" % (c, h), [P, 2 * CH], F32)
+                    res = tile("res%d_%d" % (c, h), [P, HW], F32)
                     if h == 0:
-                        nc.scalar.activation(res[:], ob[:, 0 : 2 * CH], COPY, scale=0.0625)
+                        nc.scalar.activation(res[:], ob[:, 0:HW], COPY, scale=SIXTEENTH)
                         nc.scalar.dma_start(out=rows[:, 0:2], in_=res[:].rearrange("p (a n) -> p a n", a=2))
                     else:
-                        nc.vector.tensor_scalar(res[:], ob[:, 0 : 2 * CH], 0.0625, None, MULT)
+                        nc.vector.tensor_scalar(res[:], ob[:, 0:HW], SIXTEENTH, None, MULT)
                         nc.sync.dma_start(out=rows[:, 2:4], in_=res[:].rearrange("p (a n) -> p a n", a=2))

@@ -2,7 +2,8 @@ from contextlib import ExitStack
 
 import concourse.mybir as mybir
 
-T, U = 2048, 1024
+TOKENS = 2048
+PLACES = 1024
 FLOPS = 5 * 2 * 512 * 512 * 512
 
 F32 = mybir.dt.float32
@@ -20,8 +21,12 @@ SIGMOID = mybir.ActivationFunctionType.Sigmoid
 P = 128
 PACK = 4
 W = 512
-HW = W // 2
-CH = 128
+HALF = W // 2
+CHUNK = W // PACK
+GROUP = 16
+QUADRANT = 32
+SCALE_ROWS = 16
+UPPER = 4
 SIXTEENTH = 0.0625
 
 
@@ -38,162 +43,166 @@ def tile_picked_listbias_sigmoid_p_kernel(tc, x_words, x_scales, w1, w2, gk, gq,
         def bank(b, name):
             return psum.tile([P, W], F32, name=name, tag="bank%d" % b)
 
-        def mx(name, width=W):
-            return tile(name + "_c", [P, width], U32), tile(name + "_s", [P, width], U8)
+        def operand(name, width=W):
+            return tile(name + "_words", [P, width], U32), tile(name + "_scales", [P, width], U8)
 
-        def quantize(dst, c0, src):
-            c1 = c0 + src.shape[1] // PACK
-            nc.vector.quantize_mx(out=dst[0][:, c0:c1].bitcast(FP8X4), scales=dst[1][:, c0:c1], in_=src)
+        def quantize(dst, c0, woven):
+            c1 = c0 + woven.shape[1] // PACK
+            nc.vector.quantize_mx(out=dst[0][:, c0:c1].bitcast(FP8X4), scales=dst[1][:, c0:c1], in_=woven)
 
-        def mm(o, lhs, l0, rhs, r0, n):
-            nc.tensor.matmul_mx(out=o, lhsT=lhs[0][:, l0 : l0 + P].bitcast(FP8X4), lhsT_scale=lhs[1][:, l0 : l0 + P],
+        def product(result, lhs, l0, rhs, r0, n):
+            nc.tensor.matmul_mx(out=result, lhsT=lhs[0][:, l0 : l0 + P].bitcast(FP8X4), lhsT_scale=lhs[1][:, l0 : l0 + P],
                                 rhs=rhs[0][:, r0 : r0 + n].bitcast(FP8X4), rhs_scale=rhs[1][:, r0 : r0 + n], start=True, stop=True)
 
-        def deal(dst, src):
-            nc.scalar.copy(dst, src.rearrange("p j (m t) -> p m j t", t=PACK))
+        def deal(dst, rows):
+            nc.scalar.copy(dst, rows.rearrange("p j (m t) -> p m j t", t=PACK))
 
-        def dealt(whole):
-            return whole[:].rearrange("p (t m j) -> p m j t", t=PACK, j=PACK)
+        def dealt(woven):
+            return woven[:].rearrange("p (t m j) -> p m j t", t=PACK, j=PACK)
 
-        def weigh(dst, src, gain):
-            nc.vector.tensor_tensor(dst.rearrange("p (n t) -> p n t", t=PACK), src, gain[:].unsqueeze(1).to_broadcast([P, CH, PACK]), MULT)
+        def weigh(woven, values, gain):
+            nc.vector.tensor_tensor(woven.rearrange("p (n t) -> p n t", t=PACK), values, gain[:].unsqueeze(1).to_broadcast([P, CHUNK, PACK]), MULT)
 
-        def weave(dst, src):
-            nc.scalar.copy(dst.rearrange("p (c t) -> p c t", t=PACK), src.rearrange("p t c -> p c t"))
+        def weave(woven, tiles):
+            nc.scalar.copy(woven.rearrange("p (c t) -> p c t", t=PACK), tiles.rearrange("p t c -> p c t"))
 
-        offs_t = lists.tile([P, W // 16], U16, name="offs_t")
-        qs_t = lists.tile([P, W // 16], U16, name="qs_t")
-        rel_t = lists.tile([P, W // 16], U16, name="rel_t")
+        offs_t = lists.tile([P, W // GROUP], U16, name="offs_t")
+        qs_t = lists.tile([P, W // GROUP], U16, name="qs_t")
+        rel_t = lists.tile([P, W // GROUP], U16, name="rel_t")
 
-        xw = tile("xw", [P, T], I32)
-        xs = tile("xs", [P, T], U8)
+        xw = tile("xw", [P, TOKENS], I32)
+        xs = tile("xs", [P, TOKENS], U8)
         nc.vector.memset(xs[:].bitcast(I32), 0)
         nc.sync.dma_start(qs_t[:], qs)
         nc.sync.dma_start(out=xw[:], in_=x_words[0].rearrange("p c r -> p (c r)").bitcast(I32))
-        for r in range(4):
-            nc.scalar.dma_start(out=xs[r:P:32, :].bitcast(I32), in_=x_scales[0, r:16:4, :].bitcast(I32))
         nc.sync.dma_start(offs_t[:], offs)
+        for r in range(PACK):
+            nc.sync.dma_start(out=xs[r:P:QUADRANT, :].bitcast(I32), in_=x_scales[0, r:SCALE_ROWS:PACK, :].bitcast(I32))
+
+        zeros = tile("zeros", [P, 8], F32)
+        warmed = tile("warmed", [P, 8], F32)
+        nc.gpsimd.memset(zeros[:], 0.0)
+        nc.scalar.activation(warmed[:], zeros[:], SIGMOID)
 
         gains = {}
         for name, g in (("gq", gq), ("gk", gk), ("gi", gi), ("gt", gt)):
             gains[name] = tile(name + "_t", [P, PACK], F32)
             nc.gpsimd.dma_start(out=gains[name][:], in_=g.rearrange("(p t) o -> p (t o)", t=PACK))
 
-        w2_raw = []
+        w2_rows = []
         for h in range(2):
-            w2_raw.append(tile("w2_raw%d" % h, [P, PACK, HW], F32))
-            nc.sync.dma_start(out=w2_raw[h][:], in_=w2.rearrange("(p j) c -> p j c", j=PACK)[:, :, h * HW : (h + 1) * HW])
-        raw = {}
+            w2_rows.append(tile("w2_rows%d" % h, [P, PACK, HALF], F32))
+            nc.sync.dma_start(out=w2_rows[h][:], in_=w2.rearrange("(p j) c -> p j c", j=PACK)[:, :, h * HALF : (h + 1) * HALF])
+        w_rows = {}
         for name, w in (("w1", w1), ("wv", wv)):
-            raw[name] = tile(name + "_raw", [P, PACK, W], F32)
-            nc.sync.dma_start(out=raw[name][:], in_=w.rearrange("(p j) c -> p j c", j=PACK))
+            w_rows[name] = tile(name + "_rows", [P, PACK, W], F32)
+            nc.sync.dma_start(out=w_rows[name][:], in_=w.rearrange("(p j) c -> p j c", j=PACK))
         nc.sync.dma_start(rel_t[:], rel)
         tabs = []
         for t in range(PACK):
-            tabs.append(tile("tab%d" % t, [P, U], F32))
+            tabs.append(tile("tab%d" % t, [P, PLACES], F32))
             nc.sync.dma_start(out=tabs[t][:], in_=tab.rearrange("(p t) u -> p t u", t=PACK)[:, t, :])
 
-        xk = mx("xk")
-        xq = mx("xq")
+        xk = operand("xk")
+        xq = operand("xq")
         nc.vector.tensor_copy(xq[0][:], xw[:].bitcast(U32).indirect(qs_t[:]))
-        nc.vector.tensor_copy(xq[1][:], xs[:].indirect(qs_t[:]))
         nc.vector.tensor_copy(xk[0][:].rearrange("p (t m) -> p m t", t=PACK), xw[:].bitcast(U32).indirect(offs_t[:]))
+        nc.vector.tensor_copy(xq[1][:], xs[:].indirect(qs_t[:]))
 
-        wb = {}
-        wq = {}
+        w_woven = {}
+        w_mx = {}
         for name in ("w2", "w1", "wv"):
-            wb[name] = tile(name + "_b", [P, PACK * W], BF16)
-            wq[name] = mx(name)
+            w_woven[name] = tile(name + "_woven", [P, PACK * W], BF16)
+            w_mx[name] = operand(name)
+        m_half = HALF // PACK
         for h in range(2):
-            deal(dealt(wb["w2"])[:, h * 64 : (h + 1) * 64], w2_raw[h][:])
-        quantize(wq["w2"], 0, wb["w2"][:])
-        xk_plain = tile("xk_plain", [P, W], U8, tag="w2_b")
-        nc.vector.tensor_copy(xk_plain[:], xs[:].indirect(offs_t[:]))
-        nc.vector.tensor_copy(xk[1][:].rearrange("p (t m) -> p t m", t=PACK), xk_plain[:].rearrange("p (m t) -> p t m", t=PACK))
-        deal(dealt(wb["w1"]), raw["w1"][:])
-        quantize(wq["w1"], 0, wb["w1"][:])
-        deal(dealt(wb["wv"]), raw["wv"][:])
+            deal(dealt(w_woven["w2"])[:, h * m_half : (h + 1) * m_half], w2_rows[h][:])
+        quantize(w_mx["w2"], 0, w_woven["w2"][:])
+        xk_listed = tile("xk_listed", [P, W], U8, tag="w2_woven")
+        nc.vector.tensor_copy(xk_listed[:], xs[:].indirect(offs_t[:]))
+        nc.vector.tensor_copy(xk[1][:].rearrange("p (t m) -> p t m", t=PACK), xk_listed[:].rearrange("p (m t) -> p t m", t=PACK))
+        deal(dealt(w_woven["w1"]), w_rows["w1"][:])
+        quantize(w_mx["w1"], 0, w_woven["w1"][:])
+        deal(dealt(w_woven["wv"]), w_rows["wv"][:])
 
-        z2b = [tile("z2b0", [P, 2 * W], BF16), tile("z2b1", [P, 2 * W], BF16, tag="w1_b")]
-        z2q = mx("z2")
+        z2_woven = [tile("z2_woven0", [P, PACK * HALF], BF16), tile("z2_woven1", [P, PACK * HALF], BF16, tag="w1_woven")]
+        z2 = operand("z2")
         for c in range(PACK):
-            qb = bank(4 + c, "qf%d" % c)
+            qf = bank(UPPER + c, "qf%d" % c)
             for t in range(PACK):
-                mm(qb[:, t * CH : (t + 1) * CH], wq["w2"], t * P, xq, c * CH, CH)
-            weigh(z2b[c // 2][:, c % 2 * W : (c % 2 + 1) * W], qb[:].rearrange("p (t n) -> p n t", t=PACK), gains["gq"])
+                product(qf[:, t * CHUNK : (t + 1) * CHUNK], w_mx["w2"], t * P, xq, c * CHUNK, CHUNK)
+            weigh(z2_woven[c // 2][:, c % 2 * W : (c % 2 + 1) * W], qf[:].rearrange("p (t n) -> p n t", t=PACK), gains["gq"])
 
-        zplain = tile("zplain", [P, PACK, W], BF16)
+        z_tiles = tile("z_tiles", [P, PACK, W], BF16)
         for t in range(PACK):
-            kb = bank(t, "kf%d" % t)
-            mm(kb[:], wq["w1"], t * P, xk, 0, W)
-            nc.scalar.activation(zplain[:, t, :], kb[:], COPY, scale=gains["gk"][:, t : t + 1])
-        zb = [tile("zb%d" % c, [P, W], BF16) for c in range(PACK)]
-        zq = [mx("z%d_" % c, CH) for c in range(PACK)]
-        for c in range(PACK):
-            weave(zb[c][:], zplain[:, :, c * CH : (c + 1) * CH])
+            kf = bank(t, "kf%d" % t)
+            product(kf[:], w_mx["w1"], t * P, xk, 0, W)
+            nc.scalar.activation(z_tiles[:, t, :], kf[:], COPY, scale=gains["gk"][:, t : t + 1])
+        z_woven = [tile("z_woven%d" % h, [P, PACK * HALF], BF16) for h in range(2)]
+        z = [operand("z%d" % h, HALF) for h in range(2)]
+        for h in range(2):
+            weave(z_woven[h][:], z_tiles[:, :, h * HALF : (h + 1) * HALF])
 
         for h in range(2):
-            quantize(z2q, h * HW, z2b[h][:])
-        quantize(wq["wv"], 0, wb["wv"][:])
+            quantize(z2, h * HALF, z2_woven[h][:])
+        quantize(w_mx["wv"], 0, w_woven["wv"][:])
 
-        zvb = tile("zvb", [P, PACK * W], BF16)
-        zvq = mx("zv")
-        vb = [bank(4 + c, "val%d" % c) for c in range(PACK)]
-        vplain = tile("vplain", [P, PACK, 3 * CH], BF16)
+        zv_woven = tile("zv_woven", [P, PACK * W], BF16)
+        zv = operand("zv")
+        zv_tiles = tile("zv_tiles", [P, PACK, W], BF16, tag="z_tiles")
         for t in range(PACK):
-            mm(vb[t // 2][:, t % 2 * HW : (t % 2 + 1) * HW], xk, t * P, wq["wv"], 0, HW)
-        for c in range(2, PACK):
-            for t in range(PACK):
-                mm(vb[c][:, t * CH : (t + 1) * CH], xk, t * P, wq["wv"], c * CH, CH)
-        for t in range(PACK):
-            nc.scalar.activation(vplain[:, t, 0:HW], vb[t // 2][:, t % 2 * HW : (t % 2 + 1) * HW], COPY, scale=gains["gi"][:, t : t + 1])
-        for t in range(PACK):
-            nc.scalar.activation(vplain[:, t, HW : HW + CH], vb[2][:, t * CH : (t + 1) * CH], COPY, scale=gains["gi"][:, t : t + 1])
-        weave(zvb[:, 0 : 3 * W], vplain[:])
-        weigh(zvb[:, 3 * W : 4 * W], vb[3][:].rearrange("p (t n) -> p n t", t=PACK), gains["gi"])
+            val = bank(UPPER + t, "val%d" % t)
+            product(val[:], xk, t * P, w_mx["wv"], 0, W)
+            nc.scalar.activation(zv_tiles[:, t, :], val[:], COPY, scale=gains["gi"][:, t : t + 1])
+        weave(zv_woven[:], zv_tiles[:])
 
-        bias = [tile("bias%d" % t, [P, W], F32) for t in range(PACK)]
-        pre = tile("pre", [P, PACK, W], F32)
-        for t in range(PACK):
-            quantize(zq[t], 0, zb[t][:])
-            sbk = bank(t, "s%d" % t)
-            mm(sbk[:], zq[t], 0, z2q, 0, W)
-            pieces = 2 if t == PACK - 1 else 1
-            n = W // pieces
-            for h in range(pieces):
-                nc.vector.tensor_copy(bias[t][:, h * n : (h + 1) * n], tabs[t][:].indirect(rel_t[:, h * n // 16 : (h + 1) * n // 16]))
-                nc.vector.scalar_tensor_tensor(pre[:, t, h * n : (h + 1) * n], sbk[:, h * n : (h + 1) * n], SIXTEENTH, bias[t][:, h * n : (h + 1) * n], MULT, ADD)
+        scores = []
+        for h in range(2):
+            quantize(z[h], 0, z_woven[h][:])
+            for t in (2 * h, 2 * h + 1):
+                scores.append(bank(t, "scores%d" % t))
+                product(scores[t][:], z[h], t % 2 * P, z2, 0, W)
 
-        sig = [tile("sig%d" % c, [P, W], F32) for c in range(PACK)]
+        logits = tile("logits", [P, PACK, W], F32)
+        for t in range(PACK):
+            bias = tile("bias%d" % t, [P, W], F32, tag=("bias0", "bias1", "z_woven0", "z_woven1")[t])
+            n = HALF if t == PACK - 1 else W
+            for v0 in range(0, W, n):
+                nc.vector.tensor_copy(bias[:, v0 : v0 + n], tabs[t][:].indirect(rel_t[:, v0 // GROUP : (v0 + n) // GROUP]))
+                nc.vector.scalar_tensor_tensor(logits[:, t, v0 : v0 + n], scores[t][:, v0 : v0 + n], SIXTEENTH, bias[:, v0 : v0 + n], MULT, ADD)
+
+        sigmoids = tile("sigmoids", [P, PACK * W], F32, tag="z_tiles")
+        sig = [sigmoids[:, c * W : (c + 1) * W] for c in range(PACK)]
         for c in range(PACK):
-            nc.scalar.activation(sig[c][:].rearrange("p (n i t) -> p n t i", i=4, t=PACK),
-                                 pre[:, :, c * CH : (c + 1) * CH].rearrange("p t (n i) -> p n t i", i=4), SIGMOID)
+            nc.scalar.activation(sig[c].rearrange("p (n i t) -> p n t i", i=4, t=PACK),
+                                 logits[:, :, c * CHUNK : (c + 1) * CHUNK].rearrange("p t (n i) -> p n t i", i=4), SIGMOID)
 
-        zpb = [tile("zpb%d" % c, [P, W], BF16) for c in range(PACK)]
-        zpq = [mx("zp%d_" % c, CH) for c in range(PACK)]
-        quantize(zvq, 0, zvb[:])
-        weigh(zpb[0][:], sig[0][:].rearrange("p (n t) -> p n t", t=PACK), gains["gt"])
+        zp_woven = [tile("zp_woven%d" % c, [P, W], BF16) for c in range(PACK)]
+        zp = [operand("zp%d" % c, CHUNK) for c in range(PACK)]
+        quantize(zv, 0, zv_woven[:])
+        weigh(zp_woven[0][:], sig[0].rearrange("p (n t) -> p n t", t=PACK), gains["gt"])
         for c in range(PACK):
-            if c + 1 < PACK:
-                weigh(zpb[c + 1][:], sig[c + 1][:].rearrange("p (n t) -> p n t", t=PACK), gains["gt"])
-            quantize(zpq[c], 0, zpb[c][:])
-            rows = out.rearrange("(p a) v -> p a v", a=PACK)[:, :, c * CH : (c + 1) * CH]
-            if c + 1 < PACK:
-                ob = bank(c, "o%d" % c)
+            last = c == PACK - 1
+            if not last:
+                weigh(zp_woven[c + 1][:], sig[c + 1].rearrange("p (n t) -> p n t", t=PACK), gains["gt"])
+            quantize(zp[c], 0, zp_woven[c][:])
+            rows = out.rearrange("(p a) v -> p a v", a=PACK)[:, :, c * CHUNK : (c + 1) * CHUNK]
+            if not last:
+                acc = bank(c, "out%d" % c)
                 for a in range(PACK):
-                    mm(ob[:, a * CH : (a + 1) * CH], zvq, a * P, zpq[c], 0, CH)
+                    product(acc[:, a * CHUNK : (a + 1) * CHUNK], zv, a * P, zp[c], 0, CHUNK)
                 res = tile("res%d" % c, [P, W], F32)
-                nc.scalar.activation(res[:], ob[:], COPY, scale=SIXTEENTH)
+                nc.scalar.activation(res[:], acc[:], COPY, scale=SIXTEENTH)
                 nc.sync.dma_start(out=rows, in_=res[:].rearrange("p (a n) -> p a n", a=PACK))
             else:
                 for h in range(2):
-                    ob = bank(c + 4 * h, "o%d_%d" % (c, h))
+                    acc = bank(c + UPPER * h, "out%d_%d" % (c, h))
                     for a in range(2):
-                        mm(ob[:, a * CH : (a + 1) * CH], zvq, (2 * h + a) * P, zpq[c], 0, CH)
-                    res = tile("res%d_%d" % (c, h), [P, HW], F32)
+                        product(acc[:, a * CHUNK : (a + 1) * CHUNK], zv, (2 * h + a) * P, zp[c], 0, CHUNK)
+                    res = tile("res%d_%d" % (c, h), [P, HALF], F32)
                     if h == 0:
-                        nc.scalar.activation(res[:], ob[:, 0:HW], COPY, scale=SIXTEENTH)
+                        nc.scalar.activation(res[:], acc[:, 0:HALF], COPY, scale=SIXTEENTH)
                         nc.scalar.dma_start(out=rows[:, 0:2], in_=res[:].rearrange("p (a n) -> p a n", a=2))
                     else:
-                        nc.vector.tensor_scalar(res[:], ob[:, 0:HW], SIXTEENTH, None, MULT)
+                        nc.vector.tensor_scalar(res[:], acc[:, 0:HALF], SIXTEENTH, None, MULT)
                         nc.sync.dma_start(out=rows[:, 2:4], in_=res[:].rearrange("p (a n) -> p a n", a=2))

from contextlib import ExitStack

import concourse.mybir as mybir

TOKENS = 2048
PLACES = 1024
FLOPS = 5 * 2 * 512 * 512 * 512

F32 = mybir.dt.float32
BF16 = mybir.dt.bfloat16
I32 = mybir.dt.int32
U32 = mybir.dt.uint32
U16 = mybir.dt.uint16
U8 = mybir.dt.uint8
FP8X4 = mybir.dt.float8_e4m3fn_x4
MULT = mybir.AluOpType.mult
ADD = mybir.AluOpType.add
COPY = mybir.ActivationFunctionType.Copy
SIGMOID = mybir.ActivationFunctionType.Sigmoid

P = 128
PACK = 4
W = 512
HALF = W // 2
CHUNK = W // PACK
GROUP = 16
QUADRANT = 32
SCALE_ROWS = 16
UPPER = 4
SIXTEENTH = 0.0625


def tile_picked_listbias_sigmoid_p_kernel(tc, x_words, x_scales, w1, w2, gk, gq, tab, wv, gi, gt, offs, qs, rel, out):
    nc = tc.nc
    with ExitStack() as ctx:
        lists = ctx.enter_context(tc.tile_pool(name="lists", bufs=1))
        sb = ctx.enter_context(tc.tile_pool(name="sb", bufs=1))
        psum = ctx.enter_context(tc.psum_pool(name="psum", bufs=1))

        def tile(name, shape, dtype, tag=None):
            return sb.tile(shape, dtype, name=name, tag=tag or name, align_bytes=64)

        def bank(b, name):
            return psum.tile([P, W], F32, name=name, tag="bank%d" % b)

        def operand(name, width=W):
            return tile(name + "_words", [P, width], U32), tile(name + "_scales", [P, width], U8)

        def quantize(dst, c0, woven):
            c1 = c0 + woven.shape[1] // PACK
            nc.vector.quantize_mx(out=dst[0][:, c0:c1].bitcast(FP8X4), scales=dst[1][:, c0:c1], in_=woven)

        def product(result, lhs, l0, rhs, r0, n):
            nc.tensor.matmul_mx(out=result, lhsT=lhs[0][:, l0 : l0 + P].bitcast(FP8X4), lhsT_scale=lhs[1][:, l0 : l0 + P],
                                rhs=rhs[0][:, r0 : r0 + n].bitcast(FP8X4), rhs_scale=rhs[1][:, r0 : r0 + n], start=True, stop=True)

        def deal(dst, rows):
            nc.scalar.copy(dst, rows.rearrange("p j (m t) -> p m j t", t=PACK))

        def dealt(woven):
            return woven[:].rearrange("p (t m j) -> p m j t", t=PACK, j=PACK)

        def weigh(woven, values, gain):
            nc.vector.tensor_tensor(woven.rearrange("p (n t) -> p n t", t=PACK), values, gain[:].unsqueeze(1).to_broadcast([P, CHUNK, PACK]), MULT)

        def weave(woven, tiles):
            nc.scalar.copy(woven.rearrange("p (c t) -> p c t", t=PACK), tiles.rearrange("p t c -> p c t"))

        offs_t = lists.tile([P, W // GROUP], U16, name="offs_t")
        qs_t = lists.tile([P, W // GROUP], U16, name="qs_t")
        rel_t = lists.tile([P, W // GROUP], U16, name="rel_t")

        xw = tile("xw", [P, TOKENS], I32)
        xs = tile("xs", [P, TOKENS], U8)
        nc.vector.memset(xs[:].bitcast(I32), 0)
        nc.sync.dma_start(qs_t[:], qs)
        nc.sync.dma_start(out=xw[:], in_=x_words[0].rearrange("p c r -> p (c r)").bitcast(I32))
        nc.sync.dma_start(offs_t[:], offs)
        for r in range(PACK):
            nc.sync.dma_start(out=xs[r:P:QUADRANT, :].bitcast(I32), in_=x_scales[0, r:SCALE_ROWS:PACK, :].bitcast(I32))

        zeros = tile("zeros", [P, 8], F32)
        warmed = tile("warmed", [P, 8], F32)
        nc.gpsimd.memset(zeros[:], 0.0)
        nc.scalar.activation(warmed[:], zeros[:], SIGMOID)

        gains = {}
        for name, g in (("gq", gq), ("gk", gk), ("gi", gi), ("gt", gt)):
            gains[name] = tile(name + "_t", [P, PACK], F32)
            nc.gpsimd.dma_start(out=gains[name][:], in_=g.rearrange("(p t) o -> p (t o)", t=PACK))

        w2_rows = []
        for h in range(2):
            w2_rows.append(tile("w2_rows%d" % h, [P, PACK, HALF], F32))
            nc.sync.dma_start(out=w2_rows[h][:], in_=w2.rearrange("(p j) c -> p j c", j=PACK)[:, :, h * HALF : (h + 1) * HALF])
        w_rows = {}
        for name, w in (("w1", w1), ("wv", wv)):
            w_rows[name] = tile(name + "_rows", [P, PACK, W], F32)
            nc.sync.dma_start(out=w_rows[name][:], in_=w.rearrange("(p j) c -> p j c", j=PACK))
        nc.sync.dma_start(rel_t[:], rel)
        tabs = []
        for t in range(PACK):
            tabs.append(tile("tab%d" % t, [P, PLACES], F32))
            nc.sync.dma_start(out=tabs[t][:], in_=tab.rearrange("(p t) u -> p t u", t=PACK)[:, t, :])

        xk = operand("xk")
        xq = operand("xq")
        nc.vector.tensor_copy(xq[0][:], xw[:].bitcast(U32).indirect(qs_t[:]))
        nc.vector.tensor_copy(xk[0][:].rearrange("p (t m) -> p m t", t=PACK), xw[:].bitcast(U32).indirect(offs_t[:]))
        nc.vector.tensor_copy(xq[1][:], xs[:].indirect(qs_t[:]))

        w_woven = {}
        w_mx = {}
        for name in ("w2", "w1", "wv"):
            w_woven[name] = tile(name + "_woven", [P, PACK * W], BF16)
            w_mx[name] = operand(name)
        m_half = HALF // PACK
        for h in range(2):
            deal(dealt(w_woven["w2"])[:, h * m_half : (h + 1) * m_half], w2_rows[h][:])
        quantize(w_mx["w2"], 0, w_woven["w2"][:])
        xk_listed = tile("xk_listed", [P, W], U8, tag="w2_woven")
        nc.vector.tensor_copy(xk_listed[:], xs[:].indirect(offs_t[:]))
        nc.vector.tensor_copy(xk[1][:].rearrange("p (t m) -> p t m", t=PACK), xk_listed[:].rearrange("p (m t) -> p t m", t=PACK))
        deal(dealt(w_woven["w1"]), w_rows["w1"][:])
        quantize(w_mx["w1"], 0, w_woven["w1"][:])
        deal(dealt(w_woven["wv"]), w_rows["wv"][:])

        z2_woven = [tile("z2_woven0", [P, PACK * HALF], BF16), tile("z2_woven1", [P, PACK * HALF], BF16, tag="w1_woven")]
        z2 = operand("z2")
        for c in range(PACK):
            qf = bank(UPPER + c, "qf%d" % c)
            for t in range(PACK):
                product(qf[:, t * CHUNK : (t + 1) * CHUNK], w_mx["w2"], t * P, xq, c * CHUNK, CHUNK)
            weigh(z2_woven[c // 2][:, c % 2 * W : (c % 2 + 1) * W], qf[:].rearrange("p (t n) -> p n t", t=PACK), gains["gq"])

        z_tiles = tile("z_tiles", [P, PACK, W], BF16)
        for t in range(PACK):
            kf = bank(t, "kf%d" % t)
            product(kf[:], w_mx["w1"], t * P, xk, 0, W)
            nc.scalar.activation(z_tiles[:, t, :], kf[:], COPY, scale=gains["gk"][:, t : t + 1])
        z_woven = [tile("z_woven%d" % h, [P, PACK * HALF], BF16) for h in range(2)]
        z = [operand("z%d" % h, HALF) for h in range(2)]
        for h in range(2):
            weave(z_woven[h][:], z_tiles[:, :, h * HALF : (h + 1) * HALF])

        for h in range(2):
            quantize(z2, h * HALF, z2_woven[h][:])
        quantize(w_mx["wv"], 0, w_woven["wv"][:])

        zv_woven = tile("zv_woven", [P, PACK * W], BF16)
        zv = operand("zv")
        zv_tiles = tile("zv_tiles", [P, PACK, W], BF16, tag="z_tiles")
        for t in range(PACK):
            val = bank(UPPER + t, "val%d" % t)
            product(val[:], xk, t * P, w_mx["wv"], 0, W)
            nc.scalar.activation(zv_tiles[:, t, :], val[:], COPY, scale=gains["gi"][:, t : t + 1])
        weave(zv_woven[:], zv_tiles[:])

        scores = []
        for h in range(2):
            quantize(z[h], 0, z_woven[h][:])
            for t in (2 * h, 2 * h + 1):
                scores.append(bank(t, "scores%d" % t))
                product(scores[t][:], z[h], t % 2 * P, z2, 0, W)

        logits = tile("logits", [P, PACK, W], F32)
        for t in range(PACK):
            bias = tile("bias%d" % t, [P, W], F32, tag=("bias0", "bias1", "z_woven0", "z_woven1")[t])
            n = HALF if t == PACK - 1 else W
            for v0 in range(0, W, n):
                nc.vector.tensor_copy(bias[:, v0 : v0 + n], tabs[t][:].indirect(rel_t[:, v0 // GROUP : (v0 + n) // GROUP]))
                nc.vector.scalar_tensor_tensor(logits[:, t, v0 : v0 + n], scores[t][:, v0 : v0 + n], SIXTEENTH, bias[:, v0 : v0 + n], MULT, ADD)

        sigmoids = tile("sigmoids", [P, PACK * W], F32, tag="z_tiles")
        sig = [sigmoids[:, c * W : (c + 1) * W] for c in range(PACK)]
        for c in range(PACK):
            nc.scalar.activation(sig[c].rearrange("p (n i t) -> p n t i", i=4, t=PACK),
                                 logits[:, :, c * CHUNK : (c + 1) * CHUNK].rearrange("p t (n i) -> p n t i", i=4), SIGMOID)

        zp_woven = [tile("zp_woven%d" % c, [P, W], BF16) for c in range(PACK)]
        zp = [operand("zp%d" % c, CHUNK) for c in range(PACK)]
        quantize(zv, 0, zv_woven[:])
        weigh(zp_woven[0][:], sig[0].rearrange("p (n t) -> p n t", t=PACK), gains["gt"])
        for c in range(PACK):
            last = c == PACK - 1
            if not last:
                weigh(zp_woven[c + 1][:], sig[c + 1].rearrange("p (n t) -> p n t", t=PACK), gains["gt"])
            quantize(zp[c], 0, zp_woven[c][:])
            rows = out.rearrange("(p a) v -> p a v", a=PACK)[:, :, c * CHUNK : (c + 1) * CHUNK]
            if not last:
                acc = bank(c, "out%d" % c)
                for a in range(PACK):
                    product(acc[:, a * CHUNK : (a + 1) * CHUNK], zv, a * P, zp[c], 0, CHUNK)
                res = tile("res%d" % c, [P, W], F32)
                nc.scalar.activation(res[:], acc[:], COPY, scale=SIXTEENTH)
                nc.sync.dma_start(out=rows, in_=res[:].rearrange("p (a n) -> p a n", a=PACK))
            else:
                for h in range(2):
                    acc = bank(c + UPPER * h, "out%d_%d" % (c, h))
                    for a in range(2):
                        product(acc[:, a * CHUNK : (a + 1) * CHUNK], zv, (2 * h + a) * P, zp[c], 0, CHUNK)
                    res = tile("res%d_%d" % (c, h), [P, HALF], F32)
                    if h == 0:
                        nc.scalar.activation(res[:], acc[:, 0:HALF], COPY, scale=SIXTEENTH)
                        nc.scalar.dma_start(out=rows[:, 0:2], in_=res[:].rearrange("p (a n) -> p a n", a=2))
                    else:
                        nc.vector.tensor_scalar(res[:], acc[:, 0:HALF], SIXTEENTH, None, MULT)
                        nc.sync.dma_start(out=rows[:, 2:4], in_=res[:].rearrange("p (a n) -> p a n", a=2))
